import numpy as np
import ml_dtypes


def mxq(x, axis, fmt="e4m3"):
    dtype, down = {"e4m3": (ml_dtypes.float8_e4m3fn, 7), "e5m2": (ml_dtypes.float8_e5m2, 14)}[fmt]
    v = np.moveaxis(np.asarray(x, np.float32).astype(ml_dtypes.bfloat16).astype(np.float64), axis, -1)
    blocks = v.reshape(v.shape[:-1] + (-1, 32))
    amax = np.abs(blocks).max(-1, keepdims=True)
    byte = np.maximum(np.where(amax > 0, np.frexp(amax)[1] - 1 + 127, 0) - down, 1)
    scale = np.exp2(byte - 127.0)
    codes = (blocks / scale).astype(np.float32).astype(dtype).astype(np.float64)
    return np.moveaxis((codes * scale).reshape(v.shape), -1, axis)


WIDE = False


def mx_kscale(k):
    if not WIDE:
        return np.ones(k)
    levels = np.array([10, -10, 5, -5, 0])
    if k % 512:
        return np.exp2(np.random.permutation(np.resize(levels, k // 32))).repeat(32)
    a = np.empty((k // 512, 16))
    for p in range(k // 512):
        a[p, :8] = np.random.permutation(np.resize(levels, 8))
        for g in range(8):
            far = levels[np.abs(levels - a[p, g]) >= 10]
            a[p, g + 8] = far[np.random.randint(len(far))]
    return np.exp2(a.ravel()).repeat(32)


def f64(x):
    return np.asarray(x).astype(np.float64)


def striped(idx):
    return np.tile(idx.reshape(-1, 16).T, (8, 1)).astype(np.uint16)


def unstriped(offs):
    return offs[:16].T.reshape(-1).astype(np.int64)


def pack_weight(w):
    k, n = w.shape
    w = f64(np.asarray(w, np.float32).astype(ml_dtypes.bfloat16)).reshape(k // 32, 32, n)
    amax = np.abs(w).max(1)
    byte = np.clip(np.where(amax > 0, np.frexp(amax)[1] - 1 + 127 - 7, 1), 1, 254)
    scaled = (w * np.exp2(127.0 - byte)[:, None, :]).reshape(k, n).astype(np.float32)
    words = np.ascontiguousarray(scaled.reshape(k // 512, 128, 4, n).transpose(0, 1, 3, 2)).astype(ml_dtypes.float8_e4m3fn).view(np.uint8)
    return words, np.ascontiguousarray(byte.astype(np.uint8).reshape(k // 512, 16, n))


def unpack_weight(words, scales):
    g, p, n, _ = words.shape
    vals = np.ascontiguousarray(words).view(ml_dtypes.float8_e4m3fn).astype(np.float64) * np.repeat(np.exp2(scales.astype(np.float64) - 127.0), 8, axis=1)[..., None]
    return vals.transpose(0, 1, 3, 2).reshape(g * 512, n)


K, T, E, C, N = 2560, 1024, 4, 128, 256


def by_expert(wq, xq):
    return np.concatenate([wq[e].T @ xq[:, e * C:(e + 1) * C] for e in range(E)], axis=1)


def setup_inputs():
    n = np.random.standard_normal
    s = mx_kscale(K)[:, None]
    packed = [pack_weight(m) for m in n((E, K, N)) / np.sqrt(K) / s[None]]
    return {
        "xT": (n((K, T)) * s).astype(np.float32),
        "xr": n((N, T)).astype(np.float32),
        "w_words": np.stack([m[0] for m in packed]),
        "w_scales": np.stack([m[1] for m in packed]),
        "gate": np.tile(np.random.uniform(0.2, 1.0, E * C), (N, 1)).astype(np.float32),
        "offs": striped(np.random.permutation(T)[:E * C]),
    }


def reference(xT, xr, w_words, w_scales, gate, offs):
    idx = unstriped(offs)
    w = np.stack([unpack_weight(w_words[e], w_scales[e]) for e in range(E)])
    xq = mxq(f64(xT)[:, idx], 0, "e4m3")
    y = by_expert(w, xq)
    out = f64(xr).copy()
    out[:, idx] += f64(gate) * y
    return out

@@ -1,0 +1,172 @@
+from contextlib import ExitStack
+
+import concourse.mybir as mybir
+
+K, T, E, C, N = 2560, 1024, 4, 128, 256
+SLOTS = E * C
+FLOPS = 2 * K * SLOTS * N
+
+F32 = mybir.dt.float32
+BF16 = mybir.dt.bfloat16
+I32 = mybir.dt.int32
+U32 = mybir.dt.uint32
+U16 = mybir.dt.uint16
+U8 = mybir.dt.uint8
+FP8X4 = mybir.dt.float8_e4m3fn_x4
+MULT = mybir.AluOpType.mult
+ADD = mybir.AluOpType.add
+
+P = 128
+PASSES = K // 512
+HALVES = N // P
+CHUNKS = [
+    [(0, 256, 128), (256, 256, 160), (512, 512, 384)],
+    [(0, 512, 384), (512, 512, 384)],
+    [(0, 512, 384), (512, 512, 384)],
+    [(0, 512, 384), (512, 512, 384)],
+    [(0, 512, 384), (512, 256, 160), (768, 256, 96)],
+]
+
+
+def tile_moe_res_lin_none_kernel(tc, xT, xr, w_words, w_scales, gate, offs, out):
+    nc = tc.nc
+    with ExitStack() as ctx:
+        lists = ctx.enter_context(tc.tile_pool(name="lists", bufs=1))
+        held = ctx.enter_context(tc.tile_pool(name="held", bufs=1))
+        psum = ctx.enter_context(tc.psum_pool(name="psum", bufs=1))
+
+        offsets = lists.tile([P, SLOTS // 16], U16, name="offsets")
+
+        raw, grouped, words, scales, slot_words, slot_scales = [], [], [], [], [], []
+        for a in range(PASSES):
+            raw.append(held.tile([P, 4, T], F32, name=f"raw{a}"))
+            grouped.append(held.tile([P, T, 4], BF16, name=f"grouped{a}", align_bytes=64))
+            words.append(held.tile([P, T], U32, name=f"words{a}", align_bytes=64))
+            slot_words.append(held.tile([P, SLOTS], U32, name=f"slot_words{a}", align_bytes=64))
+        w_codes = held.tile([P, E * PASSES, N], U32, name="w_codes", align_bytes=64)
+        w_bytes = held.tile([P, E * PASSES, N], U8, name="w_bytes", align_bytes=64)
+        for g in range(2):
+            scales.append(held.tile([P, T], U8, name=f"scales{g}", align_bytes=64))
+            slot_scales.append(held.tile([P, SLOTS], U8, name=f"slot_scales{g}", align_bytes=64))
+        gates = held.tile([P, SLOTS], F32, name="gates")
+        residual, placed, result = [], [], []
+        for h in range(HALVES):
+            residual.append(held.tile([P, T], F32, name=f"residual{h}"))
+            placed.append(held.tile([P, T], F32, name=f"placed{h}"))
+            result.append(held.tile([P, T], F32, name=f"result{h}"))
+
+        for g in range(2):
+            nc.gpsimd.memset(scales[g][:].bitcast(I32), 0)
+        nc.gpsimd.memset(w_bytes[:].bitcast(I32), 0)
+        for h in range(HALVES):
+            nc.gpsimd.memset(placed[h][:], 0.0)
+
+        for a in range(PASSES):
+            for c0, width, _ in CHUNKS[a]:
+                nc.sync.dma_start(
+                    raw[a][:, :, c0 : c0 + width],
+                    xT[512 * a : 512 * (a + 1), c0 : c0 + width].rearrange("(p j) w -> p j w", j=4),
+                )
+            if a == 0:
+                nc.sync.dma_start(offsets[:], offs)
+        w_rows = w_scales.rearrange("e a (q r) n -> q r (e a) n", r=4)
+        for q in range(4):
+            nc.sync.dma_start(w_bytes[32 * q : 32 * q + 4, :, :].bitcast(I32), w_rows[q].bitcast(I32))
+        for e in range(E):
+            for a0, a1 in ((0, PASSES),) if e < E - 1 else ((0, 3), (3, PASSES)):
+                nc.sync.dma_start(
+                    w_codes[:, PASSES * e + a0 : PASSES * e + a1, :].bitcast(I32),
+                    w_words[e, a0:a1].rearrange("a p n r -> p a (n r)").bitcast(I32),
+                )
+            if e == 0:
+                nc.sync.dma_start(gates[:], gate[0:P, :])
+        for h in range(HALVES):
+            nc.sync.dma_start(residual[h][:], xr[P * h : P * (h + 1), :])
+
+        def cast(engine, a, c0, c1):
+            if c1 > c0:
+                engine(
+                    grouped[a][:, c0:c1, :].rearrange("p (c i) t -> p c t i", i=4),
+                    raw[a][:, :, c0:c1].rearrange("p t (c i) -> p c t i", i=4),
+                )
+
+        def quantise(a, c0, width):
+            nc.vector.quantize_mx(
+                out=words[a][:, c0 : c0 + width].bitcast(FP8X4),
+                scales=scales[a // 4][4 * (a % 4) : P, c0 : c0 + width],
+                in_=grouped[a][:, c0 : c0 + width, :].rearrange("p c t -> p (c t)"),
+            )
+
+        def gather(a, s0, s1):
+            columns = offsets[:, s0 // 16 : s1 // 16] if s1 - s0 < SLOTS else offsets[:]
+            nc.vector.tensor_copy(slot_words[a][:, s0:s1], words[a][:].indirect(columns))
+            if a >= 3:
+                nc.vector.tensor_copy(slot_scales[a // 4][:, s0:s1], scales[a // 4][:].indirect(columns))
+
+        steps = [(a, c0, width, share) for a in range(PASSES) for c0, width, share in CHUNKS[a]]
+        for i in range(len(steps) + 1):
+            if i < len(steps):
+                a, c0, width, share = steps[i]
+                cast(nc.scalar.copy, a, c0, c0 + share)
+                cast(nc.vector.tensor_copy, a, c0 + share, c0 + width)
+            if i > 0:
+                a, c0, width, share = steps[i - 1]
+                quantise(a, c0, width)
+                if c0 + width == T and a < PASSES - 1:
+                    gather(a, 0, SLOTS)
+        for s in range(0, SLOTS, 256):
+            gather(PASSES - 1, s, s + 256)
+
+        sums = []
+        for e in range(E):
+            sums.append([])
+            for h in range(HALVES):
+                sums[e].append(psum.tile([P, C], F32, name=f"sum{e}{h}"))
+
+        def multiply(e, passes):
+            for h in range(HALVES):
+                for a in passes:
+                    nc.tensor.matmul_mx(
+                        out=sums[e][h][:],
+                        lhsT=w_codes[:, PASSES * e + a, P * h : P * (h + 1)].bitcast(FP8X4),
+                        lhsT_scale=w_bytes[:, PASSES * e + a, P * h : P * (h + 1)],
+                        rhs=slot_words[a][:, C * e : C * (e + 1)].bitcast(FP8X4),
+                        rhs_scale=slot_scales[a // 4][4 * (a % 4) : P, C * e : C * (e + 1)],
+                        start=(a == 0),
+                        stop=(a == PASSES - 1),
+                    )
+
+        early = range(PASSES - 1)
+        last = [PASSES - 1]
+        multiply(0, early)
+        multiply(1, early)
+        multiply(0, last)
+        multiply(1, last)
+        multiply(2, early)
+        multiply(2, last)
+        multiply(3, early)
+        multiply(3, last)
+
+        product = {}
+        for e in range(E):
+            for h in range(HALVES):
+                product[e, h] = held.tile([P, C], F32, name=f"product{e}{h}")
+                nc.scalar.copy(product[e, h][:], sums[e][h][:])
+
+        def place(e, h):
+            nc.vector.tensor_tensor(
+                placed[h][:].indirect(offsets[:, 8 * e : 8 * e + 8]), product[e, h][:], gates[:, C * e : C * (e + 1)], MULT
+            )
+
+        def finish(h, c0, c1):
+            nc.vector.tensor_tensor(result[h][:, c0:c1], placed[h][:, c0:c1], residual[h][:, c0:c1], ADD)
+            nc.sync.dma_start(out[P * h : P * (h + 1), c0:c1], result[h][:, c0:c1])
+
+        for e in range(E - 1):
+            for h in range(HALVES):
+                place(e, h)
+        place(3, 0)
+        finish(0, 0, T)
+        place(3, 1)
+        finish(1, 0, T // 2)
+        finish(1, T // 2, T)

@@ -19,13 +19,10 @@ ADD = mybir.AluOpType.add
 P = 128
 PASSES = K // 512
 HALVES = N // P
-CHUNKS = [
-    [(0, 256, 128), (256, 256, 160), (512, 512, 384)],
-    [(0, 512, 384), (512, 512, 384)],
-    [(0, 512, 384), (512, 512, 384)],
-    [(0, 512, 384), (512, 512, 384)],
-    [(0, 512, 384), (512, 256, 160), (768, 256, 96)],
-]
+CHUNKS = [(0, 512), (512, 512)]
+SCALAR_CASTS = [[(0, 512), (512, 256)]] * (PASSES - 1) + [[(0, 320), (512, 320)]]
+VECTOR_CASTS = [[(512, 0), (768, 256)]] * (PASSES - 1) + [[(320, 192), (832, 192)]]
+LOADS = [[(0, 512), (512, 512)]] + [[(0, T)]] * (PASSES - 2) + [[(0, 512), (512, 512)]]
 
 
 def tile_moe_res_lin_none_kernel(tc, xT, xr, w_words, w_scales, gate, offs, out):
@@ -39,7 +36,7 @@ def tile_moe_res_lin_none_kernel(tc, xT, xr, w_words, w_scales, gate, offs, out)
 
         raw, grouped, words, scales, slot_words, slot_scales = [], [], [], [], [], []
         for a in range(PASSES):
-            raw.append(held.tile([P, 4, T], F32, name=f"raw{a}"))
+            raw.append([held.tile([P, 4, width], F32, name=f"raw{a}_{c0}") for c0, width in LOADS[a]])
             grouped.append(held.tile([P, T, 4], BF16, name=f"grouped{a}", align_bytes=64))
             words.append(held.tile([P, T], U32, name=f"words{a}", align_bytes=64))
             slot_words.append(held.tile([P, SLOTS], U32, name=f"slot_words{a}", align_bytes=64))
@@ -55,40 +52,41 @@ def tile_moe_res_lin_none_kernel(tc, xT, xr, w_words, w_scales, gate, offs, out)
             placed.append(held.tile([P, T], F32, name=f"placed{h}"))
             result.append(held.tile([P, T], F32, name=f"result{h}"))
 
+        w_rows = w_scales.rearrange("e a (q r) n -> q r (e a) n", r=4)
         for g in range(2):
             nc.gpsimd.memset(scales[g][:].bitcast(I32), 0)
         nc.gpsimd.memset(w_bytes[:].bitcast(I32), 0)
+        for q in range(4):
+            nc.gpsimd.dma_start(w_bytes[32 * q : 32 * q + 4, :, :].bitcast(I32), w_rows[q].bitcast(I32))
         for h in range(HALVES):
             nc.gpsimd.memset(placed[h][:], 0.0)
 
         for a in range(PASSES):
-            for c0, width, _ in CHUNKS[a]:
+            for (c0, width), tile in zip(LOADS[a], raw[a]):
                 nc.sync.dma_start(
-                    raw[a][:, :, c0 : c0 + width],
+                    tile[:],
                     xT[512 * a : 512 * (a + 1), c0 : c0 + width].rearrange("(p j) w -> p j w", j=4),
                 )
             if a == 0:
                 nc.sync.dma_start(offsets[:], offs)
-        w_rows = w_scales.rearrange("e a (q r) n -> q r (e a) n", r=4)
-        for q in range(4):
-            nc.sync.dma_start(w_bytes[32 * q : 32 * q + 4, :, :].bitcast(I32), w_rows[q].bitcast(I32))
         for e in range(E):
+            if e == 1:
+                nc.sync.dma_start(gates[:], gate[0:P, :])
             for a0, a1 in ((0, PASSES),) if e < E - 1 else ((0, 3), (3, PASSES)):
                 nc.sync.dma_start(
                     w_codes[:, PASSES * e + a0 : PASSES * e + a1, :].bitcast(I32),
                     w_words[e, a0:a1].rearrange("a p n r -> p a (n r)").bitcast(I32),
                 )
-            if e == 0:
-                nc.sync.dma_start(gates[:], gate[0:P, :])
         for h in range(HALVES):
             nc.sync.dma_start(residual[h][:], xr[P * h : P * (h + 1), :])
 
-        def cast(engine, a, c0, c1):
-            if c1 > c0:
-                engine(
-                    grouped[a][:, c0:c1, :].rearrange("p (c i) t -> p c t i", i=4),
-                    raw[a][:, :, c0:c1].rearrange("p t (c i) -> p c t i", i=4),
-                )
+        def cast(copy, a, c0, width):
+            for (first, loaded), tile in zip(LOADS[a], raw[a]):
+                if width and first <= c0 < first + loaded:
+                    copy(
+                        grouped[a][:, c0 : c0 + width, :].rearrange("p (c i) t -> p c t i", i=4),
+                        tile[:, :, c0 - first : c0 - first + width].rearrange("p t (c i) -> p c t i", i=4),
+                    )
 
         def quantise(a, c0, width):
             nc.vector.quantize_mx(
@@ -97,25 +95,26 @@ def tile_moe_res_lin_none_kernel(tc, xT, xr, w_words, w_scales, gate, offs, out)
                 in_=grouped[a][:, c0 : c0 + width, :].rearrange("p c t -> p (c t)"),
             )
 
-        def gather(a, s0, s1):
+        def gather(target, table, s0, s1):
             columns = offsets[:, s0 // 16 : s1 // 16] if s1 - s0 < SLOTS else offsets[:]
-            nc.vector.tensor_copy(slot_words[a][:, s0:s1], words[a][:].indirect(columns))
-            if a >= 3:
-                nc.vector.tensor_copy(slot_scales[a // 4][:, s0:s1], scales[a // 4][:].indirect(columns))
+            nc.vector.tensor_copy(target[:, s0:s1], table[:].indirect(columns))
 
-        steps = [(a, c0, width, share) for a in range(PASSES) for c0, width, share in CHUNKS[a]]
-        for i in range(len(steps) + 1):
-            if i < len(steps):
-                a, c0, width, share = steps[i]
-                cast(nc.scalar.copy, a, c0, c0 + share)
-                cast(nc.vector.tensor_copy, a, c0 + share, c0 + width)
-            if i > 0:
-                a, c0, width, share = steps[i - 1]
-                quantise(a, c0, width)
-                if c0 + width == T and a < PASSES - 1:
-                    gather(a, 0, SLOTS)
-        for s in range(0, SLOTS, 256):
-            gather(PASSES - 1, s, s + 256)
+        steps = [(a, i) for a in range(PASSES) for i in range(2)]
+        for n in range(len(steps) + 1):
+            if n < len(steps):
+                a, i = steps[n]
+                cast(nc.scalar.copy, a, *SCALAR_CASTS[a][i])
+                cast(nc.vector.tensor_copy, a, *VECTOR_CASTS[a][i])
+            if n > 0:
+                a, i = steps[n - 1]
+                quantise(a, *CHUNKS[i])
+                if i == 0 and a > 0:
+                    gather(slot_words[a - 1], words[a - 1], 0, SLOTS)
+                    if a == PASSES - 1:
+                        gather(slot_scales[0], scales[0], 0, SLOTS)
+        gather(slot_words[PASSES - 1], words[PASSES - 1], 0, SLOTS)
+        gather(slot_scales[1], scales[1], 0, SLOTS // 2)
+        gather(slot_scales[1], scales[1], SLOTS // 2, SLOTS)
 
         sums = []
         for e in range(E):
@@ -136,37 +135,35 @@ def tile_moe_res_lin_none_kernel(tc, xT, xr, w_words, w_scales, gate, offs, out)
                         stop=(a == PASSES - 1),
                     )
 
-        early = range(PASSES - 1)
-        last = [PASSES - 1]
-        multiply(0, early)
-        multiply(1, early)
-        multiply(0, last)
-        multiply(1, last)
-        multiply(2, early)
-        multiply(2, last)
-        multiply(3, early)
-        multiply(3, last)
-
         product = {}
-        for e in range(E):
+
+        def weigh(e):
             for h in range(HALVES):
                 product[e, h] = held.tile([P, C], F32, name=f"product{e}{h}")
-                nc.scalar.copy(product[e, h][:], sums[e][h][:])
+                nc.vector.tensor_tensor(product[e, h][:], sums[e][h][:], gates[:, C * e : C * (e + 1)], MULT)
 
         def place(e, h):
-            nc.vector.tensor_tensor(
-                placed[h][:].indirect(offsets[:, 8 * e : 8 * e + 8]), product[e, h][:], gates[:, C * e : C * (e + 1)], MULT
-            )
+            nc.vector.tensor_copy(placed[h][:].indirect(offsets[:, 8 * e : 8 * e + 8]), product[e, h][:])
+
+        early = range(PASSES - 1)
+        last = [PASSES - 1]
+        for e in range(E - 1):
+            multiply(e, early)
+            multiply(e, last)
+        multiply(3, range(3))
+        multiply(3, range(3, PASSES))
 
         def finish(h, c0, c1):
             nc.vector.tensor_tensor(result[h][:, c0:c1], placed[h][:, c0:c1], residual[h][:, c0:c1], ADD)
             nc.sync.dma_start(out[P * h : P * (h + 1), c0:c1], result[h][:, c0:c1])
 
         for e in range(E - 1):
-            for h in range(HALVES):
-                place(e, h)
-        place(3, 0)
+            weigh(e)
+            place(e, 0)
+            place(e, 1)
+        weigh(E - 1)
+        place(E - 1, 0)
+        place(E - 1, 1)
         finish(0, 0, T)
-        place(3, 1)
         finish(1, 0, T // 2)
         finish(1, T // 2, T)

@@ -19,10 +19,9 @@ ADD = mybir.AluOpType.add
 P = 128
 PASSES = K // 512
 HALVES = N // P
-CHUNKS = [(0, 512), (512, 512)]
-SCALAR_CASTS = [[(0, 512), (512, 256)]] * (PASSES - 1) + [[(0, 320), (512, 320)]]
-VECTOR_CASTS = [[(512, 0), (768, 256)]] * (PASSES - 1) + [[(320, 192), (832, 192)]]
-LOADS = [[(0, 512), (512, 512)]] + [[(0, T)]] * (PASSES - 2) + [[(0, 512), (512, 512)]]
+LOADS = [[(0, 512), (512, 512)], [(0, T)], [(0, T)], [(0, 512), (512, 512)], [(0, 512), (512, 256), (768, 256)]]
+CHUNKS = [[(0, 512, 320), (512, 512, 320)]] * (PASSES - 1) + [[(0, 512, 320), (512, 256, 160), (768, 256, 128)]]
+PLANES = [(0, 0), (0, 4), (0, 8), (1, 0), (1, 4)]
 
 
 def tile_moe_res_lin_none_kernel(tc, xT, xr, w_words, w_scales, gate, offs, out):
@@ -55,9 +54,7 @@ def tile_moe_res_lin_none_kernel(tc, xT, xr, w_words, w_scales, gate, offs, out)
         w_rows = w_scales.rearrange("e a (q r) n -> q r (e a) n", r=4)
         for g in range(2):
             nc.gpsimd.memset(scales[g][:].bitcast(I32), 0)
-        nc.gpsimd.memset(w_bytes[:].bitcast(I32), 0)
-        for q in range(4):
-            nc.gpsimd.dma_start(w_bytes[32 * q : 32 * q + 4, :, :].bitcast(I32), w_rows[q].bitcast(I32))
+        nc.vector.memset(w_bytes[:].bitcast(I32), 0)
         for h in range(HALVES):
             nc.gpsimd.memset(placed[h][:], 0.0)
 
@@ -69,6 +66,8 @@ def tile_moe_res_lin_none_kernel(tc, xT, xr, w_words, w_scales, gate, offs, out)
                 )
             if a == 0:
                 nc.sync.dma_start(offsets[:], offs)
+        for q in range(4):
+            nc.sync.dma_start(w_bytes[32 * q : 32 * q + 4, :, :].bitcast(I32), w_rows[q].bitcast(I32))
         for e in range(E):
             if e == 1:
                 nc.sync.dma_start(gates[:], gate[0:P, :])
@@ -91,7 +90,7 @@ def tile_moe_res_lin_none_kernel(tc, xT, xr, w_words, w_scales, gate, offs, out)
         def quantise(a, c0, width):
             nc.vector.quantize_mx(
                 out=words[a][:, c0 : c0 + width].bitcast(FP8X4),
-                scales=scales[a // 4][4 * (a % 4) : P, c0 : c0 + width],
+                scales=scales[PLANES[a][0]][PLANES[a][1] : P, c0 : c0 + width],
                 in_=grouped[a][:, c0 : c0 + width, :].rearrange("p c t -> p (c t)"),
             )
 
@@ -99,18 +98,18 @@ def tile_moe_res_lin_none_kernel(tc, xT, xr, w_words, w_scales, gate, offs, out)
             columns = offsets[:, s0 // 16 : s1 // 16] if s1 - s0 < SLOTS else offsets[:]
             nc.vector.tensor_copy(target[:, s0:s1], table[:].indirect(columns))
 
-        steps = [(a, i) for a in range(PASSES) for i in range(2)]
+        steps = [(a, *chunk) for a in range(PASSES) for chunk in CHUNKS[a]]
         for n in range(len(steps) + 1):
             if n < len(steps):
-                a, i = steps[n]
-                cast(nc.scalar.copy, a, *SCALAR_CASTS[a][i])
-                cast(nc.vector.tensor_copy, a, *VECTOR_CASTS[a][i])
+                a, c0, width, share = steps[n]
+                cast(nc.scalar.copy, a, c0, share)
+                cast(nc.vector.tensor_copy, a, c0 + share, width - share)
             if n > 0:
-                a, i = steps[n - 1]
-                quantise(a, *CHUNKS[i])
-                if i == 0 and a > 0:
+                a, c0, width, share = steps[n - 1]
+                quantise(a, c0, width)
+                if c0 == 0 and a > 0:
                     gather(slot_words[a - 1], words[a - 1], 0, SLOTS)
-                    if a == PASSES - 1:
+                    if a == 3:
                         gather(slot_scales[0], scales[0], 0, SLOTS)
         gather(slot_words[PASSES - 1], words[PASSES - 1], 0, SLOTS)
         gather(slot_scales[1], scales[1], 0, SLOTS // 2)
@@ -130,7 +129,7 @@ def tile_moe_res_lin_none_kernel(tc, xT, xr, w_words, w_scales, gate, offs, out)
                         lhsT=w_codes[:, PASSES * e + a, P * h : P * (h + 1)].bitcast(FP8X4),
                         lhsT_scale=w_bytes[:, PASSES * e + a, P * h : P * (h + 1)],
                         rhs=slot_words[a][:, C * e : C * (e + 1)].bitcast(FP8X4),
-                        rhs_scale=slot_scales[a // 4][4 * (a % 4) : P, C * e : C * (e + 1)],
+                        rhs_scale=slot_scales[PLANES[a][0]][PLANES[a][1] : P, C * e : C * (e + 1)],
                         start=(a == 0),
                         stop=(a == PASSES - 1),
                     )
@@ -140,10 +139,10 @@ def tile_moe_res_lin_none_kernel(tc, xT, xr, w_words, w_scales, gate, offs, out)
         def weigh(e):
             for h in range(HALVES):
                 product[e, h] = held.tile([P, C], F32, name=f"product{e}{h}")
-                nc.vector.tensor_tensor(product[e, h][:], sums[e][h][:], gates[:, C * e : C * (e + 1)], MULT)
+                nc.scalar.copy(product[e, h][:], sums[e][h][:])
 
         def place(e, h):
-            nc.vector.tensor_copy(placed[h][:].indirect(offsets[:, 8 * e : 8 * e + 8]), product[e, h][:])
+            nc.vector.tensor_tensor(placed[h][:].indirect(offsets[:, 8 * e : 8 * e + 8]), product[e, h][:], gates[:, C * e : C * (e + 1)], MULT)
 
         early = range(PASSES - 1)
         last = [PASSES - 1]

@@ -19,8 +19,8 @@ ADD = mybir.AluOpType.add
 P = 128
 PASSES = K // 512
 HALVES = N // P
-LOADS = [[(0, 512), (512, 512)], [(0, T)], [(0, T)], [(0, 512), (512, 512)], [(0, 512), (512, 256), (768, 256)]]
-CHUNKS = [[(0, 512, 320), (512, 512, 320)]] * (PASSES - 1) + [[(0, 512, 320), (512, 256, 160), (768, 256, 128)]]
+LOADS = [[(0, T)]] * (PASSES - 1) + [[(0, 512), (512, 256), (768, 256)]]
+CHUNKS = [[(0, 512, 320), (512, 512, 320)]] * (PASSES - 1) + [[(0, 512, 320), (512, 256, 160), (768, 256, 96)]]
 PLANES = [(0, 0), (0, 4), (0, 8), (1, 0), (1, 4)]
 
 
@@ -55,6 +55,8 @@ def tile_moe_res_lin_none_kernel(tc, xT, xr, w_words, w_scales, gate, offs, out)
         for g in range(2):
             nc.gpsimd.memset(scales[g][:].bitcast(I32), 0)
         nc.vector.memset(w_bytes[:].bitcast(I32), 0)
+        for q in range(4):
+            nc.gpsimd.dma_start(w_bytes[32 * q : 32 * q + 4, :, :].bitcast(I32), w_rows[q].bitcast(I32))
         for h in range(HALVES):
             nc.gpsimd.memset(placed[h][:], 0.0)
 
@@ -66,15 +68,13 @@ def tile_moe_res_lin_none_kernel(tc, xT, xr, w_words, w_scales, gate, offs, out)
                 )
             if a == 0:
                 nc.sync.dma_start(offsets[:], offs)
-        for q in range(4):
-            nc.sync.dma_start(w_bytes[32 * q : 32 * q + 4, :, :].bitcast(I32), w_rows[q].bitcast(I32))
         for e in range(E):
             if e == 1:
                 nc.sync.dma_start(gates[:], gate[0:P, :])
-            for a0, a1 in ((0, PASSES),) if e < E - 1 else ((0, 3), (3, PASSES)):
+            for n0, n1 in ((0, N),) if e < E - 1 else ((0, P), (P, N)):
                 nc.sync.dma_start(
-                    w_codes[:, PASSES * e + a0 : PASSES * e + a1, :].bitcast(I32),
-                    w_words[e, a0:a1].rearrange("a p n r -> p a (n r)").bitcast(I32),
+                    w_codes[:, PASSES * e : PASSES * (e + 1), n0:n1].bitcast(I32),
+                    w_words[e, :, :, n0:n1, :].rearrange("a p n r -> p a (n r)").bitcast(I32),
                 )
         for h in range(HALVES):
             nc.sync.dma_start(residual[h][:], xr[P * h : P * (h + 1), :])
@@ -111,9 +111,9 @@ def tile_moe_res_lin_none_kernel(tc, xT, xr, w_words, w_scales, gate, offs, out)
                     gather(slot_words[a - 1], words[a - 1], 0, SLOTS)
                     if a == 3:
                         gather(slot_scales[0], scales[0], 0, SLOTS)
-        gather(slot_words[PASSES - 1], words[PASSES - 1], 0, SLOTS)
-        gather(slot_scales[1], scales[1], 0, SLOTS // 2)
-        gather(slot_scales[1], scales[1], SLOTS // 2, SLOTS)
+        for s in (0, SLOTS // 2):
+            gather(slot_words[PASSES - 1], words[PASSES - 1], s, s + SLOTS // 2)
+            gather(slot_scales[1], scales[1], s, s + SLOTS // 2)
 
         sums = []
         for e in range(E):
@@ -149,20 +149,22 @@ def tile_moe_res_lin_none_kernel(tc, xT, xr, w_words, w_scales, gate, offs, out)
         for e in range(E - 1):
             multiply(e, early)
             multiply(e, last)
-        multiply(3, range(3))
-        multiply(3, range(3, PASSES))
+        multiply(3, range(PASSES))
 
         def finish(h, c0, c1):
             nc.vector.tensor_tensor(result[h][:, c0:c1], placed[h][:, c0:c1], residual[h][:, c0:c1], ADD)
             nc.sync.dma_start(out[P * h : P * (h + 1), c0:c1], result[h][:, c0:c1])
 
-        for e in range(E - 1):
+        for e in range(E):
             weigh(e)
+        for e in range(E - 2):
             place(e, 0)
             place(e, 1)
-        weigh(E - 1)
-        place(E - 1, 0)
-        place(E - 1, 1)
-        finish(0, 0, T)
+        place(2, 0)
+        place(3, 0)
+        place(2, 1)
+        finish(0, 0, T // 2)
+        place(3, 1)
+        finish(0, T // 2, T)
         finish(1, 0, T // 2)
         finish(1, T // 2, T)

@@ -19,8 +19,8 @@ ADD = mybir.AluOpType.add
 P = 128
 PASSES = K // 512
 HALVES = N // P
-LOADS = [[(0, T)]] * (PASSES - 1) + [[(0, 512), (512, 256), (768, 256)]]
-CHUNKS = [[(0, 512, 320), (512, 512, 320)]] * (PASSES - 1) + [[(0, 512, 320), (512, 256, 160), (768, 256, 96)]]
+LOADS = [[(0, T)]] * (PASSES - 2) + [[(0, 512), (512, 512)]] * 2
+CHUNKS = [[(0, 512, 320), (512, 512, 320)]] * PASSES
 PLANES = [(0, 0), (0, 4), (0, 8), (1, 0), (1, 4)]
 
 
@@ -55,8 +55,6 @@ def tile_moe_res_lin_none_kernel(tc, xT, xr, w_words, w_scales, gate, offs, out)
         for g in range(2):
             nc.gpsimd.memset(scales[g][:].bitcast(I32), 0)
         nc.vector.memset(w_bytes[:].bitcast(I32), 0)
-        for q in range(4):
-            nc.gpsimd.dma_start(w_bytes[32 * q : 32 * q + 4, :, :].bitcast(I32), w_rows[q].bitcast(I32))
         for h in range(HALVES):
             nc.gpsimd.memset(placed[h][:], 0.0)
 
@@ -68,13 +66,15 @@ def tile_moe_res_lin_none_kernel(tc, xT, xr, w_words, w_scales, gate, offs, out)
                 )
             if a == 0:
                 nc.sync.dma_start(offsets[:], offs)
+        for q in range(4):
+            nc.sync.dma_start(w_bytes[32 * q : 32 * q + 4, :, :].bitcast(I32), w_rows[q].bitcast(I32))
         for e in range(E):
             if e == 1:
                 nc.sync.dma_start(gates[:], gate[0:P, :])
-            for n0, n1 in ((0, N),) if e < E - 1 else ((0, P), (P, N)):
+            for a0, a1 in ((0, 3), (3, PASSES)):
                 nc.sync.dma_start(
-                    w_codes[:, PASSES * e : PASSES * (e + 1), n0:n1].bitcast(I32),
-                    w_words[e, :, :, n0:n1, :].rearrange("a p n r -> p a (n r)").bitcast(I32),
+                    w_codes[:, PASSES * e + a0 : PASSES * e + a1, :].bitcast(I32),
+                    w_words[e, a0:a1].rearrange("a p n r -> p a (n r)").bitcast(I32),
                 )
         for h in range(HALVES):
             nc.sync.dma_start(residual[h][:], xr[P * h : P * (h + 1), :])
@@ -144,12 +144,13 @@ def tile_moe_res_lin_none_kernel(tc, xT, xr, w_words, w_scales, gate, offs, out)
         def place(e, h):
             nc.vector.tensor_tensor(placed[h][:].indirect(offsets[:, 8 * e : 8 * e + 8]), product[e, h][:], gates[:, C * e : C * (e + 1)], MULT)
 
-        early = range(PASSES - 1)
-        last = [PASSES - 1]
-        for e in range(E - 1):
-            multiply(e, early)
-            multiply(e, last)
-        multiply(3, range(PASSES))
+        for e in range(E):
+            multiply(e, range(3))
+            if e == 0:
+                multiply(e, [3])
+                multiply(e, [4])
+            else:
+                multiply(e, range(3, PASSES))
 
         def finish(h, c0, c1):
             nc.vector.tensor_tensor(result[h][:, c0:c1], placed[h][:, c0:c1], residual[h][:, c0:c1], ADD)

from contextlib import ExitStack

import concourse.mybir as mybir

K, T, E, C, N = 2560, 1024, 4, 128, 256
SLOTS = E * C
FLOPS = 2 * K * SLOTS * N

F32 = mybir.dt.float32
BF16 = mybir.dt.bfloat16
I32 = mybir.dt.int32
U32 = mybir.dt.uint32
U16 = mybir.dt.uint16
U8 = mybir.dt.uint8
FP8X4 = mybir.dt.float8_e4m3fn_x4
MULT = mybir.AluOpType.mult
ADD = mybir.AluOpType.add

P = 128
PASSES = K // 512
HALVES = N // P
LOADS = [[(0, T)]] * (PASSES - 2) + [[(0, 512), (512, 512)]] * 2
CHUNKS = [[(0, 512, 320), (512, 512, 320)]] * PASSES
PLANES = [(0, 0), (0, 4), (0, 8), (1, 0), (1, 4)]


def tile_moe_res_lin_none_kernel(tc, xT, xr, w_words, w_scales, gate, offs, out):
    nc = tc.nc
    with ExitStack() as ctx:
        lists = ctx.enter_context(tc.tile_pool(name="lists", bufs=1))
        held = ctx.enter_context(tc.tile_pool(name="held", bufs=1))
        psum = ctx.enter_context(tc.psum_pool(name="psum", bufs=1))

        offsets = lists.tile([P, SLOTS // 16], U16, name="offsets")

        raw, grouped, words, scales, slot_words, slot_scales = [], [], [], [], [], []
        for a in range(PASSES):
            raw.append([held.tile([P, 4, width], F32, name=f"raw{a}_{c0}") for c0, width in LOADS[a]])
            grouped.append(held.tile([P, T, 4], BF16, name=f"grouped{a}", align_bytes=64))
            words.append(held.tile([P, T], U32, name=f"words{a}", align_bytes=64))
            slot_words.append(held.tile([P, SLOTS], U32, name=f"slot_words{a}", align_bytes=64))
        w_codes = held.tile([P, E * PASSES, N], U32, name="w_codes", align_bytes=64)
        w_bytes = held.tile([P, E * PASSES, N], U8, name="w_bytes", align_bytes=64)
        for g in range(2):
            scales.append(held.tile([P, T], U8, name=f"scales{g}", align_bytes=64))
            slot_scales.append(held.tile([P, SLOTS], U8, name=f"slot_scales{g}", align_bytes=64))
        gates = held.tile([P, SLOTS], F32, name="gates")
        residual, placed, result = [], [], []
        for h in range(HALVES):
            residual.append(held.tile([P, T], F32, name=f"residual{h}"))
            placed.append(held.tile([P, T], F32, name=f"placed{h}"))
            result.append(held.tile([P, T], F32, name=f"result{h}"))

        w_rows = w_scales.rearrange("e a (q r) n -> q r (e a) n", r=4)
        for g in range(2):
            nc.gpsimd.memset(scales[g][:].bitcast(I32), 0)
        nc.vector.memset(w_bytes[:].bitcast(I32), 0)
        for h in range(HALVES):
            nc.gpsimd.memset(placed[h][:], 0.0)

        for a in range(PASSES):
            for (c0, width), tile in zip(LOADS[a], raw[a]):
                nc.sync.dma_start(
                    tile[:],
                    xT[512 * a : 512 * (a + 1), c0 : c0 + width].rearrange("(p j) w -> p j w", j=4),
                )
            if a == 0:
                nc.sync.dma_start(offsets[:], offs)
        for q in range(4):
            nc.sync.dma_start(w_bytes[32 * q : 32 * q + 4, :, :].bitcast(I32), w_rows[q].bitcast(I32))
        for e in range(E):
            if e == 1:
                nc.sync.dma_start(gates[:], gate[0:P, :])
            for a0, a1 in ((0, 3), (3, PASSES)):
                nc.sync.dma_start(
                    w_codes[:, PASSES * e + a0 : PASSES * e + a1, :].bitcast(I32),
                    w_words[e, a0:a1].rearrange("a p n r -> p a (n r)").bitcast(I32),
                )
        for h in range(HALVES):
            nc.sync.dma_start(residual[h][:], xr[P * h : P * (h + 1), :])

        def cast(copy, a, c0, width):
            for (first, loaded), tile in zip(LOADS[a], raw[a]):
                if width and first <= c0 < first + loaded:
                    copy(
                        grouped[a][:, c0 : c0 + width, :].rearrange("p (c i) t -> p c t i", i=4),
                        tile[:, :, c0 - first : c0 - first + width].rearrange("p t (c i) -> p c t i", i=4),
                    )

        def quantise(a, c0, width):
            nc.vector.quantize_mx(
                out=words[a][:, c0 : c0 + width].bitcast(FP8X4),
                scales=scales[PLANES[a][0]][PLANES[a][1] : P, c0 : c0 + width],
                in_=grouped[a][:, c0 : c0 + width, :].rearrange("p c t -> p (c t)"),
            )

        def gather(target, table, s0, s1):
            columns = offsets[:, s0 // 16 : s1 // 16] if s1 - s0 < SLOTS else offsets[:]
            nc.vector.tensor_copy(target[:, s0:s1], table[:].indirect(columns))

        steps = [(a, *chunk) for a in range(PASSES) for chunk in CHUNKS[a]]
        for n in range(len(steps) + 1):
            if n < len(steps):
                a, c0, width, share = steps[n]
                cast(nc.scalar.copy, a, c0, share)
                cast(nc.vector.tensor_copy, a, c0 + share, width - share)
            if n > 0:
                a, c0, width, share = steps[n - 1]
                quantise(a, c0, width)
                if c0 == 0 and a > 0:
                    gather(slot_words[a - 1], words[a - 1], 0, SLOTS)
                    if a == 3:
                        gather(slot_scales[0], scales[0], 0, SLOTS)
        for s in (0, SLOTS // 2):
            gather(slot_words[PASSES - 1], words[PASSES - 1], s, s + SLOTS // 2)
            gather(slot_scales[1], scales[1], s, s + SLOTS // 2)

        sums = []
        for e in range(E):
            sums.append([])
            for h in range(HALVES):
                sums[e].append(psum.tile([P, C], F32, name=f"sum{e}{h}"))

        def multiply(e, passes):
            for h in range(HALVES):
                for a in passes:
                    nc.tensor.matmul_mx(
                        out=sums[e][h][:],
                        lhsT=w_codes[:, PASSES * e + a, P * h : P * (h + 1)].bitcast(FP8X4),
                        lhsT_scale=w_bytes[:, PASSES * e + a, P * h : P * (h + 1)],
                        rhs=slot_words[a][:, C * e : C * (e + 1)].bitcast(FP8X4),
                        rhs_scale=slot_scales[PLANES[a][0]][PLANES[a][1] : P, C * e : C * (e + 1)],
                        start=(a == 0),
                        stop=(a == PASSES - 1),
                    )

        product = {}

        def weigh(e):
            for h in range(HALVES):
                product[e, h] = held.tile([P, C], F32, name=f"product{e}{h}")
                nc.scalar.copy(product[e, h][:], sums[e][h][:])

        def place(e, h):
            nc.vector.tensor_tensor(placed[h][:].indirect(offsets[:, 8 * e : 8 * e + 8]), product[e, h][:], gates[:, C * e : C * (e + 1)], MULT)

        for e in range(E):
            multiply(e, range(3))
            if e == 0:
                multiply(e, [3])
                multiply(e, [4])
            else:
                multiply(e, range(3, PASSES))

        def finish(h, c0, c1):
            nc.vector.tensor_tensor(result[h][:, c0:c1], placed[h][:, c0:c1], residual[h][:, c0:c1], ADD)
            nc.sync.dma_start(out[P * h : P * (h + 1), c0:c1], result[h][:, c0:c1])

        for e in range(E):
            weigh(e)
        for e in range(E - 2):
            place(e, 0)
            place(e, 1)
        place(2, 0)
        place(3, 0)
        place(2, 1)
        finish(0, 0, T // 2)
        place(3, 1)
        finish(0, T // 2, T)
        finish(1, 0, T // 2)
        finish(1, T // 2, T)
